import numpy as np
CORES = [7,14,21,28,35,42,49,56,71,78,85,92,99,106,113,120]
N = 16
ROOT = 9
WIDTHS = [1,0,12,0,64,0,12,128,0,128,128,64,12,12,12,0]
OFF = [0,1,1,13,13,77,77,89,217,217,345,473,537,549,561,573]
C = 573
def setup_inputs(rng):
    return {"x": rng.standard_normal((N, 128, C), dtype=np.float32)}
def reference(x):
    YW = max(WIDTHS)
    y = np.full((N, 128, YW), np.nan, x.dtype)
    for r in range(N):
        y[r][:, :WIDTHS[r]] = x[ROOT][:, OFF[r]:OFF[r] + WIDTHS[r]]
    return {"y": y}

@@ -1,0 +1,44 @@
+SCRATCH = {
+    "stage": ("sbuf", [128, 445], "float32"),
+    "land": ("sbuf", [128, 128], "float32"),
+}
+SEMAPHORES = ["lo", "hi", "own", "sent", "arrived", "stored"]
+
+
+def rank_program(g, core, T, topo):
+    rank = T.rank_of(core)
+    if rank is None:
+        return
+    widths, off, total = T.tables["WIDTHS"], T.tables["OFF"], T.tables["C"]
+    root = T.root
+    w = widths[rank]
+
+    if rank == root:
+        a, b = off[root], off[root] + w
+        g.sync.dma_start(T.stage[:, 0:a], T.x[:, 0:a]).then_inc(T.sem.lo, 16)
+        g.scalar.dma_start(T.stage[:, a:total - w], T.x[:, b:total]).then_inc(T.sem.hi, 16)
+        g.dma_start(T.y[:, 0:w], T.x[:, a:b]).then_inc(T.sem.own, 16)
+        sent = 0
+        for half, sem in ((0, T.sem.lo), (1, T.sem.hi)):
+            g.wait_ge(sem, 16)
+            todo = [r for r in range(len(widths)) if widths[r] > 0 and r != root and (r > root) == (half == 1)]
+            for r in sorted(todo, key=lambda r: -widths[r]):
+                dst = T.cores[r]
+                rid, pid, _se = topo.addr(dst)
+                m = topo.mask(core, dst)
+                s = off[r] if half == 0 else off[r] - w
+                g.remote_dma(T.land[:, 0:widths[r]], T.stage[:, s:s + widths[r]], T.sem.arrived, T.sem.sent,
+                             pid, rid, m)
+                sent += 8
+        g.wait_ge(T.sem.sent, sent)
+        g.wait_ge(T.sem.own, 16)
+        return
+
+    if w == 0:
+        return
+    g.wait_ge(T.sem.arrived, 8)
+    if w == 1:
+        g.dma_start(T.y[:, 0:1], T.land[:, 0:1], allow_slow_non_contiguous=True).then_inc(T.sem.stored, 16)
+    else:
+        g.dma_start(T.y[:, 0:w], T.land[:, 0:w]).then_inc(T.sem.stored, 16)
+    g.wait_ge(T.sem.stored, 16)

@@ -2,41 +2,73 @@ SCRATCH = {
     "stage": ("sbuf", [128, 445], "float32"),
     "land": ("sbuf", [128, 128], "float32"),
 }
-SEMAPHORES = ["lo", "hi", "own", "sent", "arrived", "stored"]
+SEMAPHORES = ["lo", "hi", "own", "sent", "handed", "arrived", "stored"]
+
+OFF_CHIP = 0x00FF
+ON_CHIP = 0xFF00
+ENGINES = 8
+
+
+def plan(T, topo):
+    widths, off, root = T.tables["WIDTHS"], T.tables["OFF"], T.root
+    rc = T.cores[root]
+    stage_col = [off[r] if r < root else off[r] - widths[root] for r in range(len(widths))]
+    first = topo.chip(rc) * topo.CORES_PER_CHIP
+    other_parity = (first + topo.CORES_PER_CHIP) % (topo.CHIPS * topo.CORES_PER_CHIP)
+    relays = [c for c in range(first, first + topo.CORES_PER_CHIP)
+              if topo.die(c) != topo.die(rc) and topo.may_write(c, other_parity) and T.rank_of(c) is None]
+    halves = []
+    for h, ranks in enumerate((range(0, root), range(root + 1, len(widths)))):
+        live = [r for r in ranks if widths[r] > 0]
+        direct = live[-1] if h == 0 else live[0]
+        rest = [r for r in live if r != direct]
+        assert widths[direct] == max(widths[r] for r in live)
+        block = (stage_col[rest[0]], stage_col[rest[-1]] + widths[rest[-1]])
+        halves.append((relays[h], direct, rest, block))
+    return halves, stage_col
+
+
+def send_piece(g, T, topo, r, stage_col):
+    w = T.tables["WIDTHS"][r]
+    rid, pid, _se = topo.addr(T.cores[r])
+    g.remote_dma(T.land[:, 0:w], T.stage[:, stage_col[r]:stage_col[r] + w], T.sem.arrived, T.sem.sent,
+                 pid, rid, OFF_CHIP)
 
 
 def rank_program(g, core, T, topo):
-    rank = T.rank_of(core)
-    if rank is None:
-        return
     widths, off, total = T.tables["WIDTHS"], T.tables["OFF"], T.tables["C"]
     root = T.root
-    w = widths[rank]
+    halves, stage_col = plan(T, topo)
+    rank = T.rank_of(core)
 
+    for relay, _direct, rest, _block in halves:
+        if core == relay:
+            g.wait_ge(T.sem.handed, ENGINES)
+            for r in sorted(rest, key=lambda r: -widths[r]):
+                send_piece(g, T, topo, r, stage_col)
+            g.wait_ge(T.sem.sent, ENGINES * len(rest))
+            return
+    if rank is None:
+        return
+
+    w = widths[rank]
     if rank == root:
         a, b = off[root], off[root] + w
         g.sync.dma_start(T.stage[:, 0:a], T.x[:, 0:a]).then_inc(T.sem.lo, 16)
         g.scalar.dma_start(T.stage[:, a:total - w], T.x[:, b:total]).then_inc(T.sem.hi, 16)
+        for (relay, direct, _rest, (c0, c1)), loaded in zip(halves, (T.sem.lo, T.sem.hi)):
+            g.wait_ge(loaded, 16)
+            rid, pid, _se = topo.addr(relay)
+            g.remote_dma(T.stage[:, c0:c1], T.stage[:, c0:c1], T.sem.handed, T.sem.sent, pid, rid, ON_CHIP)
+            send_piece(g, T, topo, direct, stage_col)
         g.dma_start(T.y[:, 0:w], T.x[:, a:b]).then_inc(T.sem.own, 16)
-        sent = 0
-        for half, sem in ((0, T.sem.lo), (1, T.sem.hi)):
-            g.wait_ge(sem, 16)
-            todo = [r for r in range(len(widths)) if widths[r] > 0 and r != root and (r > root) == (half == 1)]
-            for r in sorted(todo, key=lambda r: -widths[r]):
-                dst = T.cores[r]
-                rid, pid, _se = topo.addr(dst)
-                m = topo.mask(core, dst)
-                s = off[r] if half == 0 else off[r] - w
-                g.remote_dma(T.land[:, 0:widths[r]], T.stage[:, s:s + widths[r]], T.sem.arrived, T.sem.sent,
-                             pid, rid, m)
-                sent += 8
-        g.wait_ge(T.sem.sent, sent)
+        g.wait_ge(T.sem.sent, ENGINES * 2 * len(halves))
         g.wait_ge(T.sem.own, 16)
         return
 
     if w == 0:
         return
-    g.wait_ge(T.sem.arrived, 8)
+    g.wait_ge(T.sem.arrived, ENGINES)
     if w == 1:
         g.dma_start(T.y[:, 0:1], T.land[:, 0:1], allow_slow_non_contiguous=True).then_inc(T.sem.stored, 16)
     else:

SCRATCH = {
    "stage": ("sbuf", [128, 445], "float32"),
    "land": ("sbuf", [128, 128], "float32"),
}
SEMAPHORES = ["lo", "hi", "own", "sent", "handed", "arrived", "stored"]

OFF_CHIP = 0x00FF
ON_CHIP = 0xFF00
ENGINES = 8


def plan(T, topo):
    widths, off, root = T.tables["WIDTHS"], T.tables["OFF"], T.root
    rc = T.cores[root]
    stage_col = [off[r] if r < root else off[r] - widths[root] for r in range(len(widths))]
    first = topo.chip(rc) * topo.CORES_PER_CHIP
    other_parity = (first + topo.CORES_PER_CHIP) % (topo.CHIPS * topo.CORES_PER_CHIP)
    relays = [c for c in range(first, first + topo.CORES_PER_CHIP)
              if topo.die(c) != topo.die(rc) and topo.may_write(c, other_parity) and T.rank_of(c) is None]
    halves = []
    for h, ranks in enumerate((range(0, root), range(root + 1, len(widths)))):
        live = [r for r in ranks if widths[r] > 0]
        direct = live[-1] if h == 0 else live[0]
        rest = [r for r in live if r != direct]
        assert widths[direct] == max(widths[r] for r in live)
        block = (stage_col[rest[0]], stage_col[rest[-1]] + widths[rest[-1]])
        halves.append((relays[h], direct, rest, block))
    return halves, stage_col


def send_piece(g, T, topo, r, stage_col):
    w = T.tables["WIDTHS"][r]
    rid, pid, _se = topo.addr(T.cores[r])
    g.remote_dma(T.land[:, 0:w], T.stage[:, stage_col[r]:stage_col[r] + w], T.sem.arrived, T.sem.sent,
                 pid, rid, OFF_CHIP)


def rank_program(g, core, T, topo):
    widths, off, total = T.tables["WIDTHS"], T.tables["OFF"], T.tables["C"]
    root = T.root
    halves, stage_col = plan(T, topo)
    rank = T.rank_of(core)

    for relay, _direct, rest, _block in halves:
        if core == relay:
            g.wait_ge(T.sem.handed, ENGINES)
            for r in sorted(rest, key=lambda r: -widths[r]):
                send_piece(g, T, topo, r, stage_col)
            g.wait_ge(T.sem.sent, ENGINES * len(rest))
            return
    if rank is None:
        return

    w = widths[rank]
    if rank == root:
        a, b = off[root], off[root] + w
        g.sync.dma_start(T.stage[:, 0:a], T.x[:, 0:a]).then_inc(T.sem.lo, 16)
        g.scalar.dma_start(T.stage[:, a:total - w], T.x[:, b:total]).then_inc(T.sem.hi, 16)
        for (relay, direct, _rest, (c0, c1)), loaded in zip(halves, (T.sem.lo, T.sem.hi)):
            g.wait_ge(loaded, 16)
            rid, pid, _se = topo.addr(relay)
            g.remote_dma(T.stage[:, c0:c1], T.stage[:, c0:c1], T.sem.handed, T.sem.sent, pid, rid, ON_CHIP)
            send_piece(g, T, topo, direct, stage_col)
        g.dma_start(T.y[:, 0:w], T.x[:, a:b]).then_inc(T.sem.own, 16)
        g.wait_ge(T.sem.sent, ENGINES * 2 * len(halves))
        g.wait_ge(T.sem.own, 16)
        return

    if w == 0:
        return
    g.wait_ge(T.sem.arrived, ENGINES)
    if w == 1:
        g.dma_start(T.y[:, 0:1], T.land[:, 0:1], allow_slow_non_contiguous=True).then_inc(T.sem.stored, 16)
    else:
        g.dma_start(T.y[:, 0:w], T.land[:, 0:w]).then_inc(T.sem.stored, 16)
    g.wait_ge(T.sem.stored, 16)
